import numpy as np
import ml_dtypes


def mxq(x, axis, fmt="e4m3"):
    dtype, down = {"e4m3": (ml_dtypes.float8_e4m3fn, 7), "e5m2": (ml_dtypes.float8_e5m2, 14)}[fmt]
    v = np.moveaxis(np.asarray(x, np.float32).astype(ml_dtypes.bfloat16).astype(np.float64), axis, -1)
    blocks = v.reshape(v.shape[:-1] + (-1, 32))
    amax = np.abs(blocks).max(-1, keepdims=True)
    byte = np.maximum(np.where(amax > 0, np.frexp(amax)[1] - 1 + 127, 0) - down, 1)
    scale = np.exp2(byte - 127.0)
    codes = (blocks / scale).astype(np.float32).astype(dtype).astype(np.float64)
    return np.moveaxis((codes * scale).reshape(v.shape), -1, axis)


WIDE = False


def mx_kscale(k):
    if not WIDE:
        return np.ones(k)
    levels = np.array([10, -10, 5, -5, 0])
    if k % 512:
        return np.exp2(np.random.permutation(np.resize(levels, k // 32))).repeat(32)
    a = np.empty((k // 512, 16))
    for p in range(k // 512):
        a[p, :8] = np.random.permutation(np.resize(levels, 8))
        for g in range(8):
            far = levels[np.abs(levels - a[p, g]) >= 10]
            a[p, g + 8] = far[np.random.randint(len(far))]
    return np.exp2(a.ravel()).repeat(32)


BF16 = ml_dtypes.bfloat16


def bf(x):
    return np.asarray(x, np.float32).astype(BF16)


def f64(x):
    return np.asarray(x).astype(np.float64)


B, L, D, R, V = 2, 1024, 1024, 512, 512


def setup_inputs():
    s = mx_kscale(D)
    r = mx_kscale(R)
    t = mx_kscale(L)
    q = np.random.standard_normal((B, L, D)) / np.sqrt(D)
    k = np.random.standard_normal((B, L, D))
    pq = np.random.standard_normal((L, R)) / np.sqrt(R)
    pk = np.random.standard_normal((L, R))
    g = 1 + 0.1 * np.random.standard_normal((B, L))
    go = np.random.standard_normal((B, L, V)) / np.sqrt(L)
    return {"q": bf(q * s),
            "k": bf(k / s),
            "pq": bf(pq * r),
            "pk": bf(pk / r),
            "g": bf(g * t),
            "go": bf(go / t[:, None])}


def reference(q, k, pq, pk, g, go):
    content = mxq(f64(q), 2, "e4m3") @ mxq(f64(k), 2, "e4m3").swapaxes(1, 2)
    position = mxq(f64(pq), 1, "e4m3") @ mxq(f64(pk), 1, "e4m3").T
    a = np.maximum(content + position, 0.0) * f64(g)[:, :, None]
    dv = mxq(a, 1, "e4m3").swapaxes(1, 2) @ mxq(f64(go), 1, "e4m3")
    return dv

@@ -1,0 +1,222 @@
+from contextlib import ExitStack
+
+import concourse.mybir as mybir
+from concourse.masks import make_identity
+
+B, L, D, R, V = 2, 1024, 1024, 512, 512
+FLOPS = 2 * (B * L * L * D + L * L * R + B * L * L * V)
+
+F32 = mybir.dt.float32
+BF16 = mybir.dt.bfloat16
+U32 = mybir.dt.uint32
+U8 = mybir.dt.uint8
+FP8X4 = mybir.dt.float8_e4m3fn_x4
+ALU = mybir.AluOpType
+
+P = 128
+PACK = 4
+PIECE = 1024
+PART_LEAD = 5
+
+LOADS = (
+    "q00:0:2 k00:0:1 pk0:0:1 pq0:0:2 q00:2:2 k00:1:1 pk0:1:1 k00:2:2 q01:0:4 pq1:0:2 "
+    "k01:0:2 pk1:0:2 k01:2:2 go00 go01 q10:0:2 k10:0:2 q10:2:2 k10:2:2 q11:0:4 k11:0:4 go10 go11"
+)
+
+STEPS = (
+    "q00.0 q00.1 k00.0 pk0.0 pq0.0 pq0.1 q00.2 q00.3 k00.1 S000 pk0.1 k00.2 k00.3 S001 "
+    "q01.0 q01.1 q01.2 q01.3 S002 S003 pq1.0 pq1.1 k01.0 k01.1 G00.0 S010 G00.1 S011 "
+    "pk1.0 pk1.1 k01.2 k01.3 S012 G01.0 S013 G01.1 S004 "
+    "q10.0 q10.1 k10.0 k10.1 S014 F00 S005 F01 S015 S006 "
+    "q10.2 q10.3 k10.2 k10.3 S016 F02 F03 S007 G10.0 S017 F04 G10.1 S100 F05 F06 "
+    "q11.0 q11.1 q11.2 q11.3 S101 F07 S102 G11.0 S103 G11.1 "
+    "k11.0 k11.1 k11.2 k11.3 S110 S111 S112 F10 S113 F11 "
+    "S104 F12 S114 S105 F13 S115 S106 S116 S107 F14 S117 F15 F16 F17"
+)
+DIRECT = 12
+
+
+def tile_untied_position_value_gradient_s7_kernel(tc, q, k, pq, pk, g, go, out):
+    nc = tc.nc
+    with ExitStack() as ctx:
+        keep = ctx.enter_context(tc.tile_pool(name="keep", bufs=1))
+        work = ctx.enter_context(tc.tile_pool(name="work", bufs=4))
+        psum = ctx.enter_context(tc.psum_pool(name="psum", bufs=8))
+
+        ident = keep.tile([P, P], F32, name="ident")
+        make_identity(nc, ident[:])
+
+        gate = []
+        for b in range(B):
+            gate_b = keep.tile([P, 2, PACK], BF16, name="gate_%d" % b)
+            nc.scalar.dma_start(out=gate_b[:], in_=g[b].rearrange("(h p t) -> p h t", p=P, t=PACK))
+            gate.append(gate_b)
+
+        raw = {}
+        for item in LOADS.split():
+            if item.startswith("go"):
+                b, h = int(item[2]), int(item[3])
+                tile = keep.tile([P, PACK, V], BF16, name="raw_" + item, align_bytes=64)
+                nc.sync.dma_start(out=tile[:], in_=go[b, 512 * h : 512 * h + 512, :].rearrange("(p t) v -> p t v", t=PACK))
+                raw[item] = tile
+                continue
+            name, first, count = item.split(":")
+            first, count = int(first), int(count)
+            h = int(name[-1])
+            rows = slice(512 * h, 512 * h + 512)
+            if name.startswith("p"):
+                src = (pq if name[1] == "q" else pk)[rows, :]
+                slots = 2
+            else:
+                src = (q if name[0] == "q" else k)[int(name[1]), rows, :]
+                slots = 1
+            tile = keep.tile([P, count * PIECE], BF16, name="raw_%s_%d" % (name, first), align_bytes=64)
+            nc.sync.dma_start(
+                out=tile[:].rearrange("p (t k) -> p t k", t=count * slots),
+                in_=src.rearrange("(m t) k -> m t k", t=PACK)[:, first * slots : (first + count) * slots, :],
+            )
+            for n in range(count):
+                raw["%s.%d" % (name, first + n)] = tile[:, n * PIECE : n * PIECE + PIECE]
+
+        codes = {}
+        scales = {}
+        parted = {}
+        grouped = {}
+        banks = {}
+        for b in range(B):
+            for h in range(2):
+                a_code = keep.tile([P, L], U32, name="a_codes_%d%d" % (b, h), align_bytes=64)
+                a_scale = keep.tile([P, L], U8, name="a_scales_%d%d" % (b, h), align_bytes=64)
+                codes["a%d%d" % (b, h)] = a_code
+                scales["a%d%d" % (b, h)] = a_scale
+
+        def part(key):
+            tile = work.tile([P, 2, PIECE // 4], F32, name="parted", align_bytes=64, bufs=6)
+            nc.vector.tensor_copy(out=tile[:], in_=raw[key].bitcast(F32).rearrange("p (n u) -> p u n", u=2))
+            parted[key] = tile
+
+        def turn(key):
+            bank = psum.tile([P, 512], F32, name="bank")
+            for x in range(2):
+                for u in range(2):
+                    if key in parted:
+                        src = parted[key][:, u, P * x : P * x + P]
+                    else:
+                        src = raw[key].bitcast(F32)[:, 256 * x + u : 256 * x + 256 : 2]
+                    nc.tensor.transpose(bank[:, 256 * x + P * u : 256 * x + P * u + P], src, ident[:])
+            tile = work.tile([P, PIECE], BF16, name="grouped", align_bytes=64, bufs=5)
+            nc.scalar.copy(
+                out=tile[:].bitcast(F32).rearrange("p (x r u) -> p x r u", x=2, u=2),
+                in_=bank[:].rearrange("p (x u r) -> p x r u", x=2, u=2),
+            )
+            grouped[key] = tile
+
+        def quantize(key, width):
+            code = keep.tile([P, width // PACK], U32, name="codes_" + key, align_bytes=64)
+            scale = keep.tile([P, width // PACK], U8, name="scales_" + key, align_bytes=64)
+            nc.vector.quantize_mx(out=code[:].bitcast(FP8X4), scales=scale[:], in_=grouped[key][:])
+            codes[key] = code
+            scales[key] = scale
+
+        def group_go(key, half):
+            if half == 0:
+                tile = work.tile([P, PACK * V], BF16, name="go_grouped", align_bytes=64, bufs=2)
+                grouped[key] = tile
+            dst = grouped[key][:].rearrange("p (v t) -> p v t", t=PACK)
+            src = raw[key][:].rearrange("p t v -> p v t")
+            for v0 in (256 * half, 256 * half + 128):
+                nc.scalar.copy(out=dst[:, v0 : v0 + 128, :], in_=src[:, v0 : v0 + 128, :])
+
+        def score(b, h, j):
+            jh, r = divmod(j, 4)
+            bank = psum.tile([P, 512], F32, name="bank")
+            banks[b, h, j] = bank
+            for t in range(4):
+                qk, kk = "q%d%d.%d" % (b, h, t), "k%d%d.%d" % (b, jh, r)
+                passes = [
+                    (qk, 0, kk, 0),
+                    (qk, 1, kk, 1),
+                    ("pq%d.%d" % (h, t // 2), t % 2, "pk%d.%d" % (jh, r // 2), r % 2),
+                ]
+                for n, (lk, lx, rk, rx) in enumerate(passes):
+                    ls = slice(P * lx, P * lx + P)
+                    rs = slice(P * rx, P * rx + P)
+                    nc.tensor.matmul_mx(
+                        out=bank[:, P * t : P * t + P],
+                        lhsT=codes[lk][:, ls].bitcast(FP8X4),
+                        lhsT_scale=scales[lk][:, ls],
+                        rhs=codes[rk][:, rs].bitcast(FP8X4),
+                        rhs_scale=scales[rk][:, rs],
+                        start=(n == 0),
+                        stop=(n == 2),
+                    )
+
+        def gate_scores(b, h, j):
+            a_bf = work.tile([P, 512], BF16, name="a_bf", align_bytes=64, bufs=4)
+            nc.vector.scalar_tensor_tensor(
+                out=a_bf[:].rearrange("p (j t) -> p j t", t=PACK),
+                in0=banks[b, h, j][:].rearrange("p (t j) -> p j t", t=PACK),
+                scalar=0.0,
+                in1=gate[b][:, h, :].unsqueeze(1).to_broadcast([P, P, PACK]),
+                op0=ALU.max,
+                op1=ALU.mult,
+            )
+            grouped[b, h, j] = a_bf
+
+        def quantize_a(b, h, j):
+            js = slice(P * j, P * j + P)
+            key = "a%d%d" % (b, h)
+            nc.vector.quantize_mx(out=codes[key][:, js].bitcast(FP8X4), scales=scales[key][:, js], in_=grouped[b, h, j][:])
+
+        def gradient(b, j):
+            js = slice(P * j, P * j + P)
+            bank = psum.tile([P, 512], F32, name="bank")
+            for h in range(2):
+                nc.tensor.matmul_mx(
+                    out=bank[:],
+                    lhsT=codes["a%d%d" % (b, h)][:, js].bitcast(FP8X4),
+                    lhsT_scale=scales["a%d%d" % (b, h)][:, js],
+                    rhs=codes["go%d%d" % (b, h)][:].bitcast(FP8X4),
+                    rhs_scale=scales["go%d%d" % (b, h)][:],
+                    start=(h == 0),
+                    stop=(h == 1),
+                )
+            res = work.tile([P, V], F32, name="res", bufs=4)
+            jh, r = divmod(j, 4)
+            rows = out[b, 512 * jh : 512 * jh + 512, :].rearrange("(m r) v -> m r v", r=4)
+            if (b, j) == (1, 7):
+                res2 = work.tile([P, V // 2], F32, name="res2", bufs=1)
+                nc.scalar.copy(out=res[:, 0:256], in_=bank[:, 0:256])
+                nc.vector.tensor_copy(out=res2[:], in_=bank[:, 256:512])
+                nc.sync.dma_start(out=rows[:, r, 0:256], in_=res[:, 0:256])
+                nc.sync.dma_start(out=rows[:, r, 256:512], in_=res2[:])
+            else:
+                nc.scalar.copy(out=res[:], in_=bank[:])
+                nc.sync.dma_start(out=rows[:, r, :], in_=res[:])
+
+        steps = STEPS.split()
+        turns = [s for s in steps if "." in s and s[0] != "G"]
+        direct = turns[:DIRECT]
+        with tc.manual_schedule():
+            for i in range(len(steps) + 1):
+                for s in steps[i : i + PART_LEAD + 1]:
+                    if s in turns and s not in direct and s not in parted:
+                        part(s)
+                step = steps[i] if i < len(steps) else "end"
+                before = steps[i - 1] if i > 0 else "begin"
+                if step in turns:
+                    turn(step)
+                elif step[0] == "S":
+                    score(int(step[1]), int(step[2]), int(step[3]))
+                elif step[0] == "F":
+                    gradient(int(step[1]), int(step[2]))
+                elif step[0] == "G":
+                    group_go("go" + step[1:3], int(step[4]))
+                if before[0] == "S":
+                    quantize_a(int(before[1]), int(before[2]), int(before[3]))
+                if step[0] == "S":
+                    gate_scores(int(step[1]), int(step[2]), int(step[3]))
+                if before in turns:
+                    quantize(before, PIECE)
+                elif before[0] == "G" and before[4] == "1":
+                    quantize("go" + before[1:3], PACK * V)

@@ -16,24 +16,26 @@ ALU = mybir.AluOpType
 P = 128
 PACK = 4
 PIECE = 1024
-PART_LEAD = 5
+PART_LEAD = 6
 
 LOADS = (
-    "q00:0:2 k00:0:1 pk0:0:1 pq0:0:2 q00:2:2 k00:1:1 pk0:1:1 k00:2:2 q01:0:4 pq1:0:2 "
-    "k01:0:2 pk1:0:2 k01:2:2 go00 go01 q10:0:2 k10:0:2 q10:2:2 k10:2:2 q11:0:4 k11:0:4 go10 go11"
+    "q00:0:1 k00:0:1 pk0:0:1 pq0:0:1 q00:1:1 k00:1:1 q00:2:1 pq0:1:1 gate q00:3:1 k00:2:1 pk0:1:1 k00:3:1 q01:0:4 pq1:0:2 "
+    "k01:0:1 pk1:0:1 k01:1:1 k01:2:1 pk1:1:1 k01:3:1 go00 go01 q10:0:2 k10:0:2 q10:2:2 k10:2:2 q11:0:4 k11:0:4 go10 go11"
 )
 
 STEPS = (
-    "q00.0 q00.1 k00.0 pk0.0 pq0.0 pq0.1 q00.2 q00.3 k00.1 S000 pk0.1 k00.2 k00.3 S001 "
-    "q01.0 q01.1 q01.2 q01.3 S002 S003 pq1.0 pq1.1 k01.0 k01.1 G00.0 S010 G00.1 S011 "
-    "pk1.0 pk1.1 k01.2 k01.3 S012 G01.0 S013 G01.1 S004 "
-    "q10.0 q10.1 k10.0 k10.1 S014 F00 S005 F01 S015 S006 "
-    "q10.2 q10.3 k10.2 k10.3 S016 F02 F03 S007 G10.0 S017 F04 G10.1 S100 F05 F06 "
+    "q00.0 k00.0 pk0.0 pq0.0 q00.1 k00.1 q00.2 A000 pq0.1 q00.3 A001 k00.2 pk0.1 B000 k00.3 q01.0 B001 "
+    "q01.1 q01.2 S002 q01.3 pq1.0 S003 pq1.1 k01.0 pk1.0 k01.1 S010 S011 "
+    "k01.2 pk1.1 k01.3 S012 G00.0 S013 G00.1 S004 G01.0 S014 G01.1 "
+    "q10.0 q10.1 k10.0 k10.1 S005 S015 F00 S006 F01 S016 "
+    "q10.2 q10.3 k10.2 k10.3 F02 S007 F03 G10.0 S017 F04 G10.1 S100 F05 F06 "
     "q11.0 q11.1 q11.2 q11.3 S101 F07 S102 G11.0 S103 G11.1 "
     "k11.0 k11.1 k11.2 k11.3 S110 S111 S112 F10 S113 F11 "
     "S104 F12 S114 S105 F13 S115 S106 S116 S107 F14 S117 F15 F16 F17"
 )
 DIRECT = 12
+HEAD_STEPS = 32
+HEAD_LEAD = 2
 
 
 def tile_untied_position_value_gradient_s7_kernel(tc, q, k, pq, pk, g, go, out):
@@ -46,14 +48,20 @@ def tile_untied_position_value_gradient_s7_kernel(tc, q, k, pq, pk, g, go, out):
         ident = keep.tile([P, P], F32, name="ident")
         make_identity(nc, ident[:])
 
+        warm = keep.tile([P, 1], F32, name="warm")
+        nc.vector.memset(warm[:], 0.0)
+        nc.scalar.copy(out=warm[:], in_=warm[:])
+
         gate = []
-        for b in range(B):
-            gate_b = keep.tile([P, 2, PACK], BF16, name="gate_%d" % b)
-            nc.scalar.dma_start(out=gate_b[:], in_=g[b].rearrange("(h p t) -> p h t", p=P, t=PACK))
-            gate.append(gate_b)
 
         raw = {}
         for item in LOADS.split():
+            if item == "gate":
+                for b in range(B):
+                    gate_b = keep.tile([P, 2, PACK], BF16, name="gate_%d" % b)
+                    nc.sync.dma_start(out=gate_b[:], in_=g[b].rearrange("(h p t) -> p h t", p=P, t=PACK))
+                    gate.append(gate_b)
+                continue
             if item.startswith("go"):
                 b, h = int(item[2]), int(item[3])
                 tile = keep.tile([P, PACK, V], BF16, name="raw_" + item, align_bytes=64)
@@ -91,7 +99,7 @@ def tile_untied_position_value_gradient_s7_kernel(tc, q, k, pq, pk, g, go, out):
                 scales["a%d%d" % (b, h)] = a_scale
 
         def part(key):
-            tile = work.tile([P, 2, PIECE // 4], F32, name="parted", align_bytes=64, bufs=6)
+            tile = work.tile([P, 2, PIECE // 4], F32, name="parted", align_bytes=64, bufs=7)
             nc.vector.tensor_copy(out=tile[:], in_=raw[key].bitcast(F32).rearrange("p (n u) -> p u n", u=2))
             parted[key] = tile
 
@@ -127,11 +135,13 @@ def tile_untied_position_value_gradient_s7_kernel(tc, q, k, pq, pk, g, go, out):
             for v0 in (256 * half, 256 * half + 128):
                 nc.scalar.copy(out=dst[:, v0 : v0 + 128, :], in_=src[:, v0 : v0 + 128, :])
 
-        def score(b, h, j):
+        def score(b, h, j, slots):
             jh, r = divmod(j, 4)
-            bank = psum.tile([P, 512], F32, name="bank")
-            banks[b, h, j] = bank
-            for t in range(4):
+            if 0 in slots:
+                bank = psum.tile([P, 512], F32, name="bank")
+                banks[b, h, j] = bank
+            bank = banks[b, h, j]
+            for t in slots:
                 qk, kk = "q%d%d.%d" % (b, h, t), "k%d%d.%d" % (b, jh, r)
                 passes = [
                     (qk, 0, kk, 0),
@@ -199,22 +209,24 @@ def tile_untied_position_value_gradient_s7_kernel(tc, q, k, pq, pk, g, go, out):
         direct = turns[:DIRECT]
         with tc.manual_schedule():
             for i in range(len(steps) + 1):
-                for s in steps[i : i + PART_LEAD + 1]:
+                lead = HEAD_LEAD if i < HEAD_STEPS else PART_LEAD
+                for s in steps[i : i + lead + 1]:
                     if s in turns and s not in direct and s not in parted:
                         part(s)
                 step = steps[i] if i < len(steps) else "end"
                 before = steps[i - 1] if i > 0 else "begin"
                 if step in turns:
                     turn(step)
-                elif step[0] == "S":
-                    score(int(step[1]), int(step[2]), int(step[3]))
+                elif step[0] in "SAB":
+                    slots = {"S": (0, 1, 2, 3), "A": (0, 1), "B": (2, 3)}[step[0]]
+                    score(int(step[1]), int(step[2]), int(step[3]), slots)
                 elif step[0] == "F":
                     gradient(int(step[1]), int(step[2]))
                 elif step[0] == "G":
                     group_go("go" + step[1:3], int(step[4]))
-                if before[0] == "S":
+                if before[0] in "SB":
                     quantize_a(int(before[1]), int(before[2]), int(before[3]))
-                if step[0] == "S":
+                if step[0] in "SB":
                     gate_scores(int(step[1]), int(step[2]), int(step[3]))
                 if before in turns:
                     quantize(before, PIECE)

@@ -16,26 +16,23 @@ ALU = mybir.AluOpType
 P = 128
 PACK = 4
 PIECE = 1024
-PART_LEAD = 6
-
-LOADS = (
-    "q00:0:1 k00:0:1 pk0:0:1 pq0:0:1 q00:1:1 k00:1:1 q00:2:1 pq0:1:1 gate q00:3:1 k00:2:1 pk0:1:1 k00:3:1 q01:0:4 pq1:0:2 "
-    "k01:0:1 pk1:0:1 k01:1:1 k01:2:1 pk1:1:1 k01:3:1 go00 go01 q10:0:2 k10:0:2 q10:2:2 k10:2:2 q11:0:4 k11:0:4 go10 go11"
-)
 
 STEPS = (
-    "q00.0 k00.0 pk0.0 pq0.0 q00.1 k00.1 q00.2 A000 pq0.1 q00.3 A001 k00.2 pk0.1 B000 k00.3 q01.0 B001 "
-    "q01.1 q01.2 S002 q01.3 pq1.0 S003 pq1.1 k01.0 pk1.0 k01.1 S010 S011 "
-    "k01.2 pk1.1 k01.3 S012 G00.0 S013 G00.1 S004 G01.0 S014 G01.1 "
-    "q10.0 q10.1 k10.0 k10.1 S005 S015 F00 S006 F01 S016 "
-    "q10.2 q10.3 k10.2 k10.3 F02 S007 F03 G10.0 S017 F04 G10.1 S100 F05 F06 "
-    "q11.0 q11.1 q11.2 q11.3 S101 F07 S102 G11.0 S103 G11.1 "
-    "k11.0 k11.1 k11.2 k11.3 S110 S111 S112 F10 S113 F11 "
-    "S104 F12 S114 S105 F13 S115 S106 S116 S107 F14 S117 F15 F16 F17"
+    "q00.0 k00.0 pk0.0 pq0.0 q00.1 q00.2 pq0.1 q00.3 k00.1 S000 "
+    "k00.2 pk0.1 k00.3 k01.01 pk1.01 q01.01 S001 S002 S003 "
+    "q01.23 pq1.01 k01.23 S004 S005 G00.0 S010 S011 S012 G00.1 S013 S014 S015 "
+    "q10.01 k10.01 q10.23 k10.23 q11.01 G01.0 S006 S016 G01.1 S007 S017 S100 "
+    "q11.23 k11.01 k11.23 S101 F00 S102 G10.0 F01 S103 F02 G10.1 S110 F03 S111 G11.0 S112 F04 G11.1 S113 "
+    "S104 F05 S114 S105 F06 S115 F07 S106 F10 S116 S107 F11 S117 F12 F13 F14 F15 F16 F17"
 )
 DIRECT = 12
-HEAD_STEPS = 32
+PART_ON_SCALAR = ("q10.01", "q10.23", "q11.01", "k11.01")
+OUT_ON_VECTOR = ("F13", "F15")
+HEAD_STEPS = 14
 HEAD_LEAD = 2
+PART_LEAD = 4
+QUANT_LAG = 1
+GATE_LAG = 2
 
 
 def tile_untied_position_value_gradient_s7_kernel(tc, q, k, pq, pk, g, go, out):
@@ -55,36 +52,43 @@ def tile_untied_position_value_gradient_s7_kernel(tc, q, k, pq, pk, g, go, out):
         gate = []
 
         raw = {}
-        for item in LOADS.split():
-            if item == "gate":
-                for b in range(B):
-                    gate_b = keep.tile([P, 2, PACK], BF16, name="gate_%d" % b)
-                    nc.sync.dma_start(out=gate_b[:], in_=g[b].rearrange("(h p t) -> p h t", p=P, t=PACK))
-                    gate.append(gate_b)
-                continue
-            if item.startswith("go"):
-                b, h = int(item[2]), int(item[3])
-                tile = keep.tile([P, PACK, V], BF16, name="raw_" + item, align_bytes=64)
-                nc.sync.dma_start(out=tile[:], in_=go[b, 512 * h : 512 * h + 512, :].rearrange("(p t) v -> p t v", t=PACK))
-                raw[item] = tile
-                continue
-            name, first, count = item.split(":")
-            first, count = int(first), int(count)
+        steps = STEPS.split()
+        turns = [s for s in steps if "." in s and s[0] != "G"]
+
+        def load_go(key):
+            b, h = int(key[2]), int(key[3])
+            tile = keep.tile([P, PACK, V], BF16, name="raw_" + key, align_bytes=64)
+            nc.sync.dma_start(out=tile[:], in_=go[b, 512 * h : 512 * h + 512, :].rearrange("(p t) v -> p t v", t=PACK))
+            raw[key] = tile
+
+        def load_turn(key):
+            name, digits = key.split(".")
+            first, count = int(digits[0]), len(digits)
             h = int(name[-1])
             rows = slice(512 * h, 512 * h + 512)
-            if name.startswith("p"):
+            if name[0] == "p":
                 src = (pq if name[1] == "q" else pk)[rows, :]
                 slots = 2
             else:
                 src = (q if name[0] == "q" else k)[int(name[1]), rows, :]
                 slots = 1
-            tile = keep.tile([P, count * PIECE], BF16, name="raw_%s_%d" % (name, first), align_bytes=64)
+            tile = keep.tile([P, count * PIECE], BF16, name="raw_" + key, align_bytes=64)
             nc.sync.dma_start(
                 out=tile[:].rearrange("p (t k) -> p t k", t=count * slots),
                 in_=src.rearrange("(m t) k -> m t k", t=PACK)[:, first * slots : (first + count) * slots, :],
             )
-            for n in range(count):
-                raw["%s.%d" % (name, first + n)] = tile[:, n * PIECE : n * PIECE + PIECE]
+            raw[key] = tile
+
+        for n, step in enumerate(steps):
+            if step in turns:
+                load_turn(step)
+            elif step[0] == "G" and step[4] == "0":
+                load_go("go" + step[1:3])
+            elif step == "S000":
+                for b in range(B):
+                    gate_b = keep.tile([P, 2, PACK], BF16, name="gate_%d" % b)
+                    nc.sync.dma_start(out=gate_b[:], in_=g[b].rearrange("(h p t) -> p h t", p=P, t=PACK))
+                    gate.append(gate_b)
 
         codes = {}
         scales = {}
@@ -99,32 +103,44 @@ def tile_untied_position_value_gradient_s7_kernel(tc, q, k, pq, pk, g, go, out):
                 scales["a%d%d" % (b, h)] = a_scale
 
         def part(key):
-            tile = work.tile([P, 2, PIECE // 4], F32, name="parted", align_bytes=64, bufs=7)
-            nc.vector.tensor_copy(out=tile[:], in_=raw[key].bitcast(F32).rearrange("p (n u) -> p u n", u=2))
+            count = len(key.split(".")[1])
+            tile = work.tile([P, 2, 2 * PIECE // 4], F32, name="parted", align_bytes=64, bufs=4)
+            copy = nc.scalar.copy if key in PART_ON_SCALAR else nc.vector.tensor_copy
+            copy(out=tile[:, :, 0 : count * PIECE // 4], in_=raw[key][:].bitcast(F32).rearrange("p (n u) -> p u n", u=2))
             parted[key] = tile
 
         def turn(key):
-            bank = psum.tile([P, 512], F32, name="bank")
-            for x in range(2):
-                for u in range(2):
-                    if key in parted:
-                        src = parted[key][:, u, P * x : P * x + P]
-                    else:
-                        src = raw[key].bitcast(F32)[:, 256 * x + u : 256 * x + 256 : 2]
-                    nc.tensor.transpose(bank[:, 256 * x + P * u : 256 * x + P * u + P], src, ident[:])
-            tile = work.tile([P, PIECE], BF16, name="grouped", align_bytes=64, bufs=5)
-            nc.scalar.copy(
-                out=tile[:].bitcast(F32).rearrange("p (x r u) -> p x r u", x=2, u=2),
-                in_=bank[:].rearrange("p (x u r) -> p x r u", x=2, u=2),
-            )
+            count = len(key.split(".")[1])
+            tile = work.tile([P, 2 * PIECE], BF16, name="grouped", align_bytes=64, bufs=4)
+            for n in range(count):
+                bank = psum.tile([P, 512], F32, name="bank")
+                for x in range(2):
+                    for u in range(2):
+                        w = 2 * n + x
+                        if key in parted:
+                            src = parted[key][:, u, P * w : P * w + P]
+                        else:
+                            src = raw[key][:].bitcast(F32)[:, 256 * w + u : 256 * w + 256 : 2]
+                        nc.tensor.transpose(bank[:, 256 * x + P * u : 256 * x + P * u + P], src, ident[:])
+                nc.scalar.copy(
+                    out=tile[:, PIECE * n : PIECE * n + PIECE].bitcast(F32).rearrange("p (x r u) -> p x r u", x=2, u=2),
+                    in_=bank[:].rearrange("p (x u r) -> p x r u", x=2, u=2),
+                )
             grouped[key] = tile
 
         def quantize(key, width):
             code = keep.tile([P, width // PACK], U32, name="codes_" + key, align_bytes=64)
             scale = keep.tile([P, width // PACK], U8, name="scales_" + key, align_bytes=64)
-            nc.vector.quantize_mx(out=code[:].bitcast(FP8X4), scales=scale[:], in_=grouped[key][:])
-            codes[key] = code
-            scales[key] = scale
+            nc.vector.quantize_mx(out=code[:].bitcast(FP8X4), scales=scale[:], in_=grouped[key][:, 0:width])
+            if key in turns:
+                name, digits = key.split(".")
+                for n, d in enumerate(digits):
+                    cols = slice(PIECE // PACK * n, PIECE // PACK * n + PIECE // PACK)
+                    codes["%s.%s" % (name, d)] = code[:, cols]
+                    scales["%s.%s" % (name, d)] = scale[:, cols]
+            else:
+                codes[key] = code
+                scales[key] = scale
 
         def group_go(key, half):
             if half == 0:
@@ -132,16 +148,14 @@ def tile_untied_position_value_gradient_s7_kernel(tc, q, k, pq, pk, g, go, out):
                 grouped[key] = tile
             dst = grouped[key][:].rearrange("p (v t) -> p v t", t=PACK)
             src = raw[key][:].rearrange("p t v -> p v t")
-            for v0 in (256 * half, 256 * half + 128):
-                nc.scalar.copy(out=dst[:, v0 : v0 + 128, :], in_=src[:, v0 : v0 + 128, :])
+            vs = slice(256 * half, 256 * half + 256)
+            nc.scalar.copy(out=dst[:, vs, :], in_=src[:, vs, :])
 
-        def score(b, h, j, slots):
+        def score(b, h, j):
             jh, r = divmod(j, 4)
-            if 0 in slots:
-                bank = psum.tile([P, 512], F32, name="bank")
-                banks[b, h, j] = bank
-            bank = banks[b, h, j]
-            for t in slots:
+            bank = psum.tile([P, 512], F32, name="bank")
+            banks[b, h, j] = bank
+            for t in range(4):
                 qk, kk = "q%d%d.%d" % (b, h, t), "k%d%d.%d" % (b, jh, r)
                 passes = [
                     (qk, 0, kk, 0),
@@ -201,34 +215,32 @@ def tile_untied_position_value_gradient_s7_kernel(tc, q, k, pq, pk, g, go, out):
                 nc.sync.dma_start(out=rows[:, r, 0:256], in_=res[:, 0:256])
                 nc.sync.dma_start(out=rows[:, r, 256:512], in_=res2[:])
             else:
-                nc.scalar.copy(out=res[:], in_=bank[:])
+                copy = nc.vector.tensor_copy if "F%d%d" % (b, j) in OUT_ON_VECTOR else nc.scalar.copy
+                copy(out=res[:], in_=bank[:])
                 nc.sync.dma_start(out=rows[:, r, :], in_=res[:])
 
-        steps = STEPS.split()
-        turns = [s for s in steps if "." in s and s[0] != "G"]
         direct = turns[:DIRECT]
         with tc.manual_schedule():
-            for i in range(len(steps) + 1):
+            for i in range(len(steps)):
                 lead = HEAD_LEAD if i < HEAD_STEPS else PART_LEAD
                 for s in steps[i : i + lead + 1]:
                     if s in turns and s not in direct and s not in parted:
                         part(s)
-                step = steps[i] if i < len(steps) else "end"
-                before = steps[i - 1] if i > 0 else "begin"
+                step = steps[i]
                 if step in turns:
                     turn(step)
-                elif step[0] in "SAB":
-                    slots = {"S": (0, 1, 2, 3), "A": (0, 1), "B": (2, 3)}[step[0]]
-                    score(int(step[1]), int(step[2]), int(step[3]), slots)
+                elif step[0] == "S":
+                    score(int(step[1]), int(step[2]), int(step[3]))
+                    gate_scores(int(step[1]), int(step[2]), int(step[3]))
                 elif step[0] == "F":
                     gradient(int(step[1]), int(step[2]))
                 elif step[0] == "G":
                     group_go("go" + step[1:3], int(step[4]))
-                if before[0] in "SB":
-                    quantize_a(int(before[1]), int(before[2]), int(before[3]))
-                if step[0] in "SB":
-                    gate_scores(int(step[1]), int(step[2]), int(step[3]))
-                if before in turns:
-                    quantize(before, PIECE)
-                elif before[0] == "G" and before[4] == "1":
-                    quantize("go" + before[1:3], PACK * V)
+                old = steps[i - GATE_LAG] if i >= GATE_LAG else "begin"
+                if old[0] == "S":
+                    quantize_a(int(old[1]), int(old[2]), int(old[3]))
+                old = steps[i - QUANT_LAG] if i >= QUANT_LAG else "begin"
+                if old in turns:
+                    quantize(old, len(old.split(".")[1]) * PIECE)
+                elif old[0] == "G" and old[4] == "1":
+                    quantize("go" + old[1:3], PACK * V)

@@ -16,27 +16,26 @@ ALU = mybir.AluOpType
 P = 128
 PACK = 4
 PIECE = 1024
+RING = 10
 
 STEPS = (
-    "q00.0 k00.0 pk0.0 pq0.0 q00.1 q00.2 pq0.1 q00.3 k00.1 S000 "
-    "k00.2 pk0.1 k00.3 k01.01 pk1.01 q01.01 S001 S002 S003 "
-    "q01.23 pq1.01 k01.23 S004 S005 G00.0 S010 S011 S012 G00.1 S013 S014 S015 "
-    "q10.01 k10.01 q10.23 k10.23 q11.01 G01.0 S006 S016 G01.1 S007 S017 S100 "
-    "q11.23 k11.01 k11.23 S101 F00 S102 G10.0 F01 S103 F02 G10.1 S110 F03 S111 G11.0 S112 F04 G11.1 S113 "
-    "S104 F05 S114 S105 F06 S115 F07 S106 F10 S116 S107 F11 S117 F12 F13 F14 F15 F16 F17"
+    "p:pk0.0 P:k00.0 q00.0 pk0.0 P:pq0.0 P:q00.1 k00.0 pq0.0 P:pq0.1 P:pk0.1 q00.1 q00.2 pq0.1 q00.3 k00.1 pk0.1 pk1.01 k00.2 "
+    "S000 S001 p:q01.23 P:k00.3 P:pq1.01 q01.01 q01.23 k00.3 pq1.01 P:k01.23 k01.01 S002 k01.23 G00.0 S003 G00.1 S004 S005 "
+    "P:q10.01 S010 S011 S012 G01.0 p:q10.23 G01.1 S013 p:k10.23 p:q11.23 S006 P:k10.01 S007 S014 P:q11.01 "
+    "q10.01 P:k11.01 k10.01 q10.23 k10.23 q11.01 Q00 q11.23 Q01 k11.01 k11.23 S015 G10.0 G10.1 S016 G11.0 S017 "
+    "W100.0 W100.1 F00 F01 F02 W100.2 W100.3 W110.0 i100.0 I100.1 W110.1 F03 A100.0 A100.1 W110.2 G11.1 W110.3 "
+    "W101.0 i110.0 F04 Q10 W101.1 i110.1 W101.2 A110.0 A110.1 W101.3 F05 i101.0 F06 Q11 S114 i101.1 F07 S115 "
+    "A101.0 A101.1 F10 F11 F12 F13 S116 S117 F14 F15 F16 F17"
 )
-DIRECT = 12
-PART_ON_SCALAR = ("q10.01", "q10.23", "q11.01", "k11.01")
-OUT_ON_VECTOR = ("F13", "F15")
-HEAD_STEPS = 14
-HEAD_LEAD = 2
-PART_LEAD = 4
-QUANT_LAG = 1
-GATE_LAG = 2
+WIDE = ("k10.01", "k10.23", "k11.01", "k11.23")
+OUT_ON_VECTOR = ("F07", "F10", "F16")
 
 
 def tile_untied_position_value_gradient_s7_kernel(tc, q, k, pq, pk, g, go, out):
     nc = tc.nc
+    steps = STEPS.split()
+    turns = [s for s in steps if s[0] in "qkp" and s[1] != ":"]
+    parts = [s[2:] for s in steps if s[1] == ":"]
     with ExitStack() as ctx:
         keep = ctx.enter_context(tc.tile_pool(name="keep", bufs=1))
         work = ctx.enter_context(tc.tile_pool(name="work", bufs=4))
@@ -49,52 +48,58 @@ def tile_untied_position_value_gradient_s7_kernel(tc, q, k, pq, pk, g, go, out):
         nc.vector.memset(warm[:], 0.0)
         nc.scalar.copy(out=warm[:], in_=warm[:])
 
-        gate = []
-
         raw = {}
-        steps = STEPS.split()
-        turns = [s for s in steps if "." in s and s[0] != "G"]
-
-        def load_go(key):
-            b, h = int(key[2]), int(key[3])
-            tile = keep.tile([P, PACK, V], BF16, name="raw_" + key, align_bytes=64)
-            nc.sync.dma_start(out=tile[:], in_=go[b, 512 * h : 512 * h + 512, :].rearrange("(p t) v -> p t v", t=PACK))
-            raw[key] = tile
-
-        def load_turn(key):
-            name, digits = key.split(".")
-            first, count = int(digits[0]), len(digits)
-            h = int(name[-1])
-            rows = slice(512 * h, 512 * h + 512)
-            if name[0] == "p":
-                src = (pq if name[1] == "q" else pk)[rows, :]
-                slots = 2
-            else:
-                src = (q if name[0] == "q" else k)[int(name[1]), rows, :]
-                slots = 1
-            tile = keep.tile([P, count * PIECE], BF16, name="raw_" + key, align_bytes=64)
-            nc.sync.dma_start(
-                out=tile[:].rearrange("p (t k) -> p t k", t=count * slots),
-                in_=src.rearrange("(m t) k -> m t k", t=PACK)[:, first * slots : (first + count) * slots, :],
-            )
-            raw[key] = tile
-
-        for n, step in enumerate(steps):
-            if step in turns:
-                load_turn(step)
-            elif step[0] == "G" and step[4] == "0":
-                load_go("go" + step[1:3])
-            elif step == "S000":
-                for b in range(B):
-                    gate_b = keep.tile([P, 2, PACK], BF16, name="gate_%d" % b)
-                    nc.sync.dma_start(out=gate_b[:], in_=g[b].rearrange("(h p t) -> p h t", p=P, t=PACK))
-                    gate.append(gate_b)
-
         codes = {}
         scales = {}
         parted = {}
         grouped = {}
         banks = {}
+        gate = []
+
+        def load(key):
+            digits = key.split(".")[1] if "." in key else "0000"
+            if len(digits) == 1:
+                tile = keep.tile([P, PIECE], BF16, name="raw_" + key, align_bytes=64)
+            else:
+                tile = work.tile([P, 2 * PIECE], BF16, name="raw", align_bytes=64, bufs=RING)
+            if key[0] == "g":
+                h = int(key[3])
+                src = go[int(key[2]), 512 * h : 512 * h + 512, :].rearrange("(p t) v -> p t v", t=PACK)
+            else:
+                name = key.split(".")[0]
+                h = int(name[-1])
+                rows = slice(512 * h, 512 * h + 512)
+                if name[0] == "p":
+                    src = (pq if name[1] == "q" else pk)[rows, :]
+                    slots = 2
+                else:
+                    src = (q if name[0] == "q" else k)[int(name[1]), rows, :]
+                    slots = 1
+                first, last = slots * int(digits[0]), slots * int(digits[-1]) + slots
+                src = src.rearrange("(m t) k -> m t k", t=PACK)[:, first:last, :]
+            nc.sync.dma_start(out=tile[:].rearrange("p (t k) -> p t k", t=src.shape[1]), in_=src)
+            raw[key] = tile
+
+        pending = []
+        for s in steps:
+            if s in turns:
+                pending.append(s)
+            elif s[0] == "G" and s[4] == "0":
+                pending.append("go" + s[1:3])
+
+        def load_next():
+            if pending:
+                load(pending.pop(0))
+
+        for n in range(12 + RING):
+            load_next()
+            if n == 7:
+                for b in range(B):
+                    gate_bf = keep.tile([P, 2, PACK], BF16, name="gate_bf_%d" % b)
+                    nc.sync.dma_start(out=gate_bf[:], in_=g[b].rearrange("(h p t) -> p h t", p=P, t=PACK))
+                    gate_b = keep.tile([P, 2, PACK], F32, name="gate_%d" % b)
+                    gate.append((gate_bf, gate_b))
+
         for b in range(B):
             for h in range(2):
                 a_code = keep.tile([P, L], U32, name="a_codes_%d%d" % (b, h), align_bytes=64)
@@ -102,12 +107,34 @@ def tile_untied_position_value_gradient_s7_kernel(tc, q, k, pq, pk, g, go, out):
                 codes["a%d%d" % (b, h)] = a_code
                 scales["a%d%d" % (b, h)] = a_scale
 
-        def part(key):
+        columns = {}
+        whole = {}
+
+        def code_tiles(key, width):
+            code = keep.tile([P, width], U32, name="codes_" + key, align_bytes=64)
+            scale = keep.tile([P, width], U8, name="scales_" + key, align_bytes=64)
+            return code, scale
+
+        for name in ("k10", "k11"):
+            pair = code_tiles(name, 1024)
+            for c in range(2):
+                whole[name, c] = pair + (512 * c,)
+                for r in range(4):
+                    columns["%s.%d" % (name, r), c] = pair + (512 * c + P * r,)
+        for name in ("pk0", "pk1"):
+            pair = code_tiles(name, 512)
+            whole[name, 0] = pair + (0,)
+            for n in range(2):
+                for x in range(2):
+                    columns["%s.%d" % (name, n), x] = pair + (256 * n + P * x,)
+
+        def part(key, copy):
             count = len(key.split(".")[1])
-            tile = work.tile([P, 2, 2 * PIECE // 4], F32, name="parted", align_bytes=64, bufs=4)
-            copy = nc.scalar.copy if key in PART_ON_SCALAR else nc.vector.tensor_copy
+            tile = work.tile([P, 2, PIECE // 2], F32, name="parted", align_bytes=64, bufs=7)
             copy(out=tile[:, :, 0 : count * PIECE // 4], in_=raw[key][:].bitcast(F32).rearrange("p (n u) -> p u n", u=2))
             parted[key] = tile
+            if count == 2:
+                load_next()
 
         def turn(key):
             count = len(key.split(".")[1])
@@ -116,8 +143,8 @@ def tile_untied_position_value_gradient_s7_kernel(tc, q, k, pq, pk, g, go, out):
                 bank = psum.tile([P, 512], F32, name="bank")
                 for x in range(2):
                     for u in range(2):
-                        w = 2 * n + x
-                        if key in parted:
+                        w = 2 * x + n if key in WIDE else 2 * n + x
+                        if key in parts:
                             src = parted[key][:, u, P * w : P * w + P]
                         else:
                             src = raw[key][:].bitcast(F32)[:, 256 * w + u : 256 * w + 256 : 2]
@@ -127,120 +154,151 @@ def tile_untied_position_value_gradient_s7_kernel(tc, q, k, pq, pk, g, go, out):
                     in_=bank[:].rearrange("p (x u r) -> p x r u", x=2, u=2),
                 )
             grouped[key] = tile
+            if count == 2 and key not in parts:
+                load_next()
 
-        def quantize(key, width):
-            code = keep.tile([P, width // PACK], U32, name="codes_" + key, align_bytes=64)
-            scale = keep.tile([P, width // PACK], U8, name="scales_" + key, align_bytes=64)
-            nc.vector.quantize_mx(out=code[:].bitcast(FP8X4), scales=scale[:], in_=grouped[key][:, 0:width])
-            if key in turns:
-                name, digits = key.split(".")
+        def quantize(src, place, width):
+            code, scale, first = place
+            cols = slice(first, first + width // PACK)
+            nc.vector.quantize_mx(out=code[:, cols].bitcast(FP8X4), scales=scale[:, cols], in_=src)
+
+        def quantize_turn(key):
+            name, digits = key.split(".")
+            width = len(digits) * PIECE
+            src = grouped[key]
+            if key in WIDE:
+                for c in range(2):
+                    quantize(src[:, PIECE * c : PIECE * c + PIECE], columns["%s.%s" % (name, digits[0]), c], PIECE)
+                return
+            if ("%s.%s" % (name, digits[0]), 0) not in columns:
+                pair = code_tiles(key, width // PACK)
                 for n, d in enumerate(digits):
-                    cols = slice(PIECE // PACK * n, PIECE // PACK * n + PIECE // PACK)
-                    codes["%s.%s" % (name, d)] = code[:, cols]
-                    scales["%s.%s" % (name, d)] = scale[:, cols]
-            else:
-                codes[key] = code
-                scales[key] = scale
+                    for x in range(2):
+                        columns["%s.%s" % (name, d), x] = pair + (256 * n + P * x,)
+            quantize(src[:, 0:width], columns["%s.%s" % (name, digits[0]), 0], width)
 
-        def group_go(key, half):
-            if half == 0:
-                tile = work.tile([P, PACK * V], BF16, name="go_grouped", align_bytes=64, bufs=2)
+        def interleave(key, src, half, copy):
+            if key not in grouped:
+                tile = work.tile([P, PACK * 512], BF16, name="interleaved", align_bytes=64, bufs=3)
                 grouped[key] = tile
-            dst = grouped[key][:].rearrange("p (v t) -> p v t", t=PACK)
-            src = raw[key][:].rearrange("p t v -> p v t")
-            vs = slice(256 * half, 256 * half + 256)
-            nc.scalar.copy(out=dst[:, vs, :], in_=src[:, vs, :])
+            cols = slice(256 * half, 256 * half + 256)
+            dst = grouped[key][:].rearrange("p (c t) -> p c t", t=PACK)
+            copy(out=dst[:, cols, :], in_=src.rearrange("p (t c) -> p c t", t=PACK)[:, cols, :])
+
+        def mx(out_ap, lhs, rhs, n, start, stop):
+            lc, lscale, l0 = lhs
+            rc, rscale, r0 = rhs
+            nc.tensor.matmul_mx(
+                out=out_ap,
+                lhsT=lc[:, l0 : l0 + P].bitcast(FP8X4),
+                lhsT_scale=lscale[:, l0 : l0 + P],
+                rhs=rc[:, r0 : r0 + n].bitcast(FP8X4),
+                rhs_scale=rscale[:, r0 : r0 + n],
+                start=start,
+                stop=stop,
+            )
+
+        def stationary(b, h, t):
+            q_key, pq_key = "q%d%d.%d" % (b, h, t), "pq%d.%d" % (h, t // 2)
+            return [columns[q_key, 0], columns[q_key, 1], columns[pq_key, t % 2]]
 
         def score(b, h, j):
             jh, r = divmod(j, 4)
             bank = psum.tile([P, 512], F32, name="bank")
-            banks[b, h, j] = bank
-            for t in range(4):
-                qk, kk = "q%d%d.%d" % (b, h, t), "k%d%d.%d" % (b, jh, r)
-                passes = [
-                    (qk, 0, kk, 0),
-                    (qk, 1, kk, 1),
-                    ("pq%d.%d" % (h, t // 2), t % 2, "pk%d.%d" % (jh, r // 2), r % 2),
-                ]
-                for n, (lk, lx, rk, rx) in enumerate(passes):
-                    ls = slice(P * lx, P * lx + P)
-                    rs = slice(P * rx, P * rx + P)
-                    nc.tensor.matmul_mx(
-                        out=bank[:, P * t : P * t + P],
-                        lhsT=codes[lk][:, ls].bitcast(FP8X4),
-                        lhsT_scale=scales[lk][:, ls],
-                        rhs=codes[rk][:, rs].bitcast(FP8X4),
-                        rhs_scale=scales[rk][:, rs],
-                        start=(n == 0),
-                        stop=(n == 2),
-                    )
-
-        def gate_scores(b, h, j):
+            k_key, pk_key = "k%d%d.%d" % (b, jh, r), "pk%d.%d" % (jh, r // 2)
+            moving = [columns[k_key, 0], columns[k_key, 1], columns[pk_key, r % 2]]
+            for t in range(PACK):
+                for n, lhs in enumerate(stationary(b, h, t)):
+                    mx(bank[:, P * t : P * t + P], lhs, moving[n], P, n == 0, n == 2)
             a_bf = work.tile([P, 512], BF16, name="a_bf", align_bytes=64, bufs=4)
             nc.vector.scalar_tensor_tensor(
                 out=a_bf[:].rearrange("p (j t) -> p j t", t=PACK),
-                in0=banks[b, h, j][:].rearrange("p (t j) -> p j t", t=PACK),
+                in0=bank[:].rearrange("p (t j) -> p j t", t=PACK),
                 scalar=0.0,
-                in1=gate[b][:, h, :].unsqueeze(1).to_broadcast([P, P, PACK]),
+                in1=gate[b][1][:, h, :].unsqueeze(1).to_broadcast([P, P, PACK]),
                 op0=ALU.max,
                 op1=ALU.mult,
             )
             grouped[b, h, j] = a_bf
 
         def quantize_a(b, h, j):
-            js = slice(P * j, P * j + P)
-            key = "a%d%d" % (b, h)
-            nc.vector.quantize_mx(out=codes[key][:, js].bitcast(FP8X4), scales=scales[key][:, js], in_=grouped[b, h, j][:])
+            quantize(grouped[b, h, j][:], (codes["a%d%d" % (b, h)], scales["a%d%d" % (b, h)], P * j), 512)
+
+        def wide_score(b, h, jh, t):
+            bank = psum.tile([P, 512], F32, name="bank")
+            moving = [whole["k%d%d" % (b, jh), 0], whole["k%d%d" % (b, jh), 1], whole["pk%d" % jh, 0]]
+            for n, lhs in enumerate(stationary(b, h, t)):
+                mx(bank[:], lhs, moving[n], 512, n == 0, n == 2)
+            if t == 0:
+                tile = work.tile([P, PACK * 512], BF16, name="parted", align_bytes=64, bufs=7)
+                parted[b, h, jh] = tile
+            nc.vector.tensor_scalar(
+                out=parted[b, h, jh][:, 512 * t : 512 * t + 512],
+                in0=bank[:],
+                scalar1=0.0,
+                scalar2=gate[b][1][:, h, t : t + 1],
+                op0=ALU.max,
+                op1=ALU.mult,
+            )
 
         def gradient(b, j):
-            js = slice(P * j, P * j + P)
-            bank = psum.tile([P, 512], F32, name="bank")
+            bank = psum.tile([P, V], F32, name="bank")
             for h in range(2):
-                nc.tensor.matmul_mx(
-                    out=bank[:],
-                    lhsT=codes["a%d%d" % (b, h)][:, js].bitcast(FP8X4),
-                    lhsT_scale=scales["a%d%d" % (b, h)][:, js],
-                    rhs=codes["go%d%d" % (b, h)][:].bitcast(FP8X4),
-                    rhs_scale=scales["go%d%d" % (b, h)][:],
-                    start=(h == 0),
-                    stop=(h == 1),
-                )
+                a_key, go_key = "a%d%d" % (b, h), "go%d%d" % (b, h)
+                mx(bank[:], (codes[a_key], scales[a_key], P * j), (codes[go_key], scales[go_key], 0), V, h == 0, h == 1)
             res = work.tile([P, V], F32, name="res", bufs=4)
             jh, r = divmod(j, 4)
-            rows = out[b, 512 * jh : 512 * jh + 512, :].rearrange("(m r) v -> m r v", r=4)
+            rows = out[b, 512 * jh : 512 * jh + 512, :].rearrange("(m r) v -> m r v", r=4)[:, r, :]
             if (b, j) == (1, 7):
                 res2 = work.tile([P, V // 2], F32, name="res2", bufs=1)
                 nc.scalar.copy(out=res[:, 0:256], in_=bank[:, 0:256])
                 nc.vector.tensor_copy(out=res2[:], in_=bank[:, 256:512])
-                nc.sync.dma_start(out=rows[:, r, 0:256], in_=res[:, 0:256])
-                nc.sync.dma_start(out=rows[:, r, 256:512], in_=res2[:])
+                nc.sync.dma_start(out=rows[:, 0:256], in_=res[:, 0:256])
+                nc.sync.dma_start(out=rows[:, 256:512], in_=res2[:])
             else:
                 copy = nc.vector.tensor_copy if "F%d%d" % (b, j) in OUT_ON_VECTOR else nc.scalar.copy
                 copy(out=res[:], in_=bank[:])
-                nc.sync.dma_start(out=rows[:, r, :], in_=res[:])
+                nc.sync.dma_start(out=rows, in_=res[:])
 
-        direct = turns[:DIRECT]
         with tc.manual_schedule():
-            for i in range(len(steps)):
-                lead = HEAD_LEAD if i < HEAD_STEPS else PART_LEAD
-                for s in steps[i : i + lead + 1]:
-                    if s in turns and s not in direct and s not in parted:
-                        part(s)
-                step = steps[i]
+            before = "-"
+            for step in steps:
+                kind = step[0]
+                d = [int(c) for c in step if c in "0123456789"]
+                if step[1] == ":":
+                    part(step[2:], nc.vector.tensor_copy if kind == "P" else nc.scalar.copy)
+                    continue
+                if kind == "G":
+                    key = "go" + step[1:3]
+                    interleave(key, raw[key][:], d[2], nc.scalar.copy)
+                    continue
+                if kind == "Q":
+                    key = "go" + step[1:3]
+                    load_next()
+                    codes[key], scales[key] = code_tiles(key, V)
+                    quantize(grouped[key][:], (codes[key], scales[key], 0), PACK * V)
+                    continue
+                if kind in "Ii":
+                    interleave(step[1:4], parted[d[0], d[1], d[2]][:], d[3], nc.vector.tensor_copy if kind == "I" else nc.scalar.copy)
+                    continue
+                if kind == "A":
+                    b, h, jh, half = d
+                    key = "a%d%d" % (b, h)
+                    quantize(grouped[step[1:4]][:, 1024 * half : 1024 * half + 1024], (codes[key], scales[key], 512 * jh + 256 * half), 1024)
+                    continue
                 if step in turns:
                     turn(step)
-                elif step[0] == "S":
-                    score(int(step[1]), int(step[2]), int(step[3]))
-                    gate_scores(int(step[1]), int(step[2]), int(step[3]))
-                elif step[0] == "F":
-                    gradient(int(step[1]), int(step[2]))
-                elif step[0] == "G":
-                    group_go("go" + step[1:3], int(step[4]))
-                old = steps[i - GATE_LAG] if i >= GATE_LAG else "begin"
-                if old[0] == "S":
-                    quantize_a(int(old[1]), int(old[2]), int(old[3]))
-                old = steps[i - QUANT_LAG] if i >= QUANT_LAG else "begin"
-                if old in turns:
-                    quantize(old, len(old.split(".")[1]) * PIECE)
-                elif old[0] == "G" and old[4] == "1":
-                    quantize("go" + old[1:3], PACK * V)
+                elif kind == "S":
+                    if step == "S000":
+                        for gate_bf, gate_b in gate:
+                            nc.vector.tensor_copy(out=gate_b[:], in_=gate_bf[:])
+                    score(d[0], d[1], d[2])
+                elif kind == "W":
+                    wide_score(d[0], d[1], d[2], d[3])
+                elif kind == "F":
+                    gradient(d[0], d[1])
+                if before[0] == "S":
+                    quantize_a(int(before[1]), int(before[2]), int(before[3]))
+                elif before in turns:
+                    quantize_turn(before)
+                before = step

@@ -15,20 +15,22 @@ ALU = mybir.AluOpType
 
 P = 128
 PACK = 4
+K_PASS = P * PACK
+HALF = 512
 PIECE = 1024
 RING = 10
 
 STEPS = (
-    "p:pk0.0 P:k00.0 q00.0 pk0.0 P:pq0.0 P:q00.1 k00.0 pq0.0 P:pq0.1 P:pk0.1 q00.1 q00.2 pq0.1 q00.3 k00.1 pk0.1 pk1.01 k00.2 "
-    "S000 S001 p:q01.23 P:k00.3 P:pq1.01 q01.01 q01.23 k00.3 pq1.01 P:k01.23 k01.01 S002 k01.23 G00.0 S003 G00.1 S004 S005 "
-    "P:q10.01 S010 S011 S012 G01.0 p:q10.23 G01.1 S013 p:k10.23 p:q11.23 S006 P:k10.01 S007 S014 P:q11.01 "
-    "q10.01 P:k11.01 k10.01 q10.23 k10.23 q11.01 Q00 q11.23 Q01 k11.01 k11.23 S015 G10.0 G10.1 S016 G11.0 S017 "
-    "W100.0 W100.1 F00 F01 F02 W100.2 W100.3 W110.0 i100.0 I100.1 W110.1 F03 A100.0 A100.1 W110.2 G11.1 W110.3 "
-    "W101.0 i110.0 F04 Q10 W101.1 i110.1 W101.2 A110.0 A110.1 W101.3 F05 i101.0 F06 Q11 S114 i101.1 F07 S115 "
-    "A101.0 A101.1 F10 F11 F12 F13 S116 S117 F14 F15 F16 F17"
+    "P:q00.1 q00.0 pk0.0 k00.0 pq0.0 P:k00.1 q00.1 q00.2 pq0.1 q00.3 k00.1 pk0.1 pk1.01 k00.2 S000 S001 "
+    "P:k00.3 P:pq1.01 q01.01 q01.23 k00.3 P:k01.23 pq1.01 k01.01 S002 k01.23 S003 G01.1 G00.0 S004 S005 S010 "
+    "G00.1 S011 S012 G01.0 S013 S006 p:q10.01 S007 S014 Q00 p:q10.23 p:q11.01 P:k11.01 P:q11.23 P:k11.23 "
+    "q10.01 k10.01 q10.23 k10.23 q11.01 q11.23 Q01 k11.01 k11.23 S015 G11.1 S016 S017 G10.1 W100.0 W100.1 "
+    "G11.0 F00 F01 F02 W100.2 W100.3 G10.0 i100.0 W110.0 W110.1 F03 W110.2 W110.3 i100.1 Q10 W101.0 i110.0 "
+    "A100.1 F04 W101.1 W101.2 W101.3 F05 A110.0 Q11 A100.0 i110.1 F06 i101.1 A110.1 S114 F07 i101.0 S115 F10 "
+    "F11 A101.0 F12 A101.1 F13 S116 S117 F14 F15 F16 F17"
 )
 WIDE = ("k10.01", "k10.23", "k11.01", "k11.23")
-OUT_ON_VECTOR = ("F07", "F10", "F16")
+OUT_ON_VECTOR = ("F07",)
 
 
 def tile_untied_position_value_gradient_s7_kernel(tc, q, k, pq, pk, g, go, out):
@@ -36,6 +38,8 @@ def tile_untied_position_value_gradient_s7_kernel(tc, q, k, pq, pk, g, go, out):
     steps = STEPS.split()
     turns = [s for s in steps if s[0] in "qkp" and s[1] != ":"]
     parts = [s[2:] for s in steps if s[1] == ":"]
+    first_score = [s for s in steps if s[0] == "S"][0]
+
     with ExitStack() as ctx:
         keep = ctx.enter_context(tc.tile_pool(name="keep", bufs=1))
         work = ctx.enter_context(tc.tile_pool(name="work", bufs=4))
@@ -49,26 +53,28 @@ def tile_untied_position_value_gradient_s7_kernel(tc, q, k, pq, pk, g, go, out):
         nc.scalar.copy(out=warm[:], in_=warm[:])
 
         raw = {}
-        codes = {}
-        scales = {}
         parted = {}
         grouped = {}
+        codes = {}
+        scales = {}
+        columns = {}
         banks = {}
+        whole = {}
         gate = []
 
         def load(key):
-            digits = key.split(".")[1] if "." in key else "0000"
+            digits = key.split(".")[1] if "." in key else "01"
             if len(digits) == 1:
                 tile = keep.tile([P, PIECE], BF16, name="raw_" + key, align_bytes=64)
             else:
                 tile = work.tile([P, 2 * PIECE], BF16, name="raw", align_bytes=64, bufs=RING)
             if key[0] == "g":
                 h = int(key[3])
-                src = go[int(key[2]), 512 * h : 512 * h + 512, :].rearrange("(p t) v -> p t v", t=PACK)
+                src = go[int(key[2]), HALF * h : HALF * h + HALF, :].rearrange("(p t) v -> p t v", t=PACK)
             else:
                 name = key.split(".")[0]
                 h = int(name[-1])
-                rows = slice(512 * h, 512 * h + 512)
+                rows = slice(HALF * h, HALF * h + HALF)
                 if name[0] == "p":
                     src = (pq if name[1] == "q" else pk)[rows, :]
                     slots = 2
@@ -76,86 +82,94 @@ def tile_untied_position_value_gradient_s7_kernel(tc, q, k, pq, pk, g, go, out):
                     src = (q if name[0] == "q" else k)[int(name[1]), rows, :]
                     slots = 1
                 first, last = slots * int(digits[0]), slots * int(digits[-1]) + slots
-                src = src.rearrange("(m t) k -> m t k", t=PACK)[:, first:last, :]
-            nc.sync.dma_start(out=tile[:].rearrange("p (t k) -> p t k", t=src.shape[1]), in_=src)
+                src = src.rearrange("(m s) k -> m s k", s=PACK)[:, first:last, :]
+            nc.sync.dma_start(out=tile[:].rearrange("p (s k) -> p s k", s=src.shape[1]), in_=src)
             raw[key] = tile
 
         pending = []
         for s in steps:
             if s in turns:
                 pending.append(s)
-            elif s[0] == "G" and s[4] == "0":
+            elif s[0] in "GH" and "go" + s[1:3] not in pending:
                 pending.append("go" + s[1:3])
+        singles = [s for s in turns if len(s.split(".")[1]) == 1]
+
+        ring = []
+        read = set()
 
         def load_next():
             if pending:
-                load(pending.pop(0))
+                key = pending.pop(0)
+                load(key)
+                if key not in singles:
+                    ring.append(key)
 
-        for n in range(12 + RING):
+        def has_been_read(key):
+            read.add(key)
+            while ring and ring[0] in read:
+                ring.pop(0)
+                load_next()
+
+        for n in range(len(singles) + RING):
             load_next()
             if n == 7:
                 for b in range(B):
                     gate_bf = keep.tile([P, 2, PACK], BF16, name="gate_bf_%d" % b)
-                    nc.sync.dma_start(out=gate_bf[:], in_=g[b].rearrange("(h p t) -> p h t", p=P, t=PACK))
+                    nc.sync.dma_start(out=gate_bf[:], in_=g[b].rearrange("(h p s) -> p h s", p=P, s=PACK))
                     gate_b = keep.tile([P, 2, PACK], F32, name="gate_%d" % b)
                     gate.append((gate_bf, gate_b))
-
-        for b in range(B):
-            for h in range(2):
-                a_code = keep.tile([P, L], U32, name="a_codes_%d%d" % (b, h), align_bytes=64)
-                a_scale = keep.tile([P, L], U8, name="a_scales_%d%d" % (b, h), align_bytes=64)
-                codes["a%d%d" % (b, h)] = a_code
-                scales["a%d%d" % (b, h)] = a_scale
-
-        columns = {}
-        whole = {}
 
         def code_tiles(key, width):
             code = keep.tile([P, width], U32, name="codes_" + key, align_bytes=64)
             scale = keep.tile([P, width], U8, name="scales_" + key, align_bytes=64)
             return code, scale
 
+        for b in range(B):
+            for h in range(2):
+                key = "a%d%d" % (b, h)
+                codes[key], scales[key] = code_tiles(key, L)
         for name in ("k10", "k11"):
-            pair = code_tiles(name, 1024)
+            pair = code_tiles(name, 2 * HALF)
             for c in range(2):
-                whole[name, c] = pair + (512 * c,)
-                for r in range(4):
-                    columns["%s.%d" % (name, r), c] = pair + (512 * c + P * r,)
+                whole[name, c] = pair + (HALF * c,)
+                for s in range(PACK):
+                    columns["%s.%d" % (name, s), c] = pair + (HALF * c + P * s,)
         for name in ("pk0", "pk1"):
-            pair = code_tiles(name, 512)
+            pair = code_tiles(name, HALF)
             whole[name, 0] = pair + (0,)
             for n in range(2):
                 for x in range(2):
-                    columns["%s.%d" % (name, n), x] = pair + (256 * n + P * x,)
+                    columns["%s.%d" % (name, n), x] = pair + (P * (2 * n + x),)
 
         def part(key, copy):
-            count = len(key.split(".")[1])
+            pairs = len(key.split(".")[1]) * PIECE // 4
             tile = work.tile([P, 2, PIECE // 2], F32, name="parted", align_bytes=64, bufs=7)
-            copy(out=tile[:, :, 0 : count * PIECE // 4], in_=raw[key][:].bitcast(F32).rearrange("p (n u) -> p u n", u=2))
+            copy(
+                out=tile[:, :, 0:pairs].rearrange("p u (c w) -> p c u w", c=2),
+                in_=raw[key][:].bitcast(F32).rearrange("p (c w u) -> p c u w", c=2, u=2),
+            )
             parted[key] = tile
-            if count == 2:
-                load_next()
+            has_been_read(key)
 
         def turn(key):
-            count = len(key.split(".")[1])
             tile = work.tile([P, 2 * PIECE], BF16, name="grouped", align_bytes=64, bufs=4)
-            for n in range(count):
+            for n in range(len(key.split(".")[1])):
                 bank = psum.tile([P, 512], F32, name="bank")
                 for x in range(2):
+                    w = 2 * x + n if key in WIDE else 2 * n + x
                     for u in range(2):
-                        w = 2 * x + n if key in WIDE else 2 * n + x
                         if key in parts:
                             src = parted[key][:, u, P * w : P * w + P]
                         else:
                             src = raw[key][:].bitcast(F32)[:, 256 * w + u : 256 * w + 256 : 2]
                         nc.tensor.transpose(bank[:, 256 * x + P * u : 256 * x + P * u + P], src, ident[:])
                 nc.scalar.copy(
-                    out=tile[:, PIECE * n : PIECE * n + PIECE].bitcast(F32).rearrange("p (x r u) -> p x r u", x=2, u=2),
-                    in_=bank[:].rearrange("p (x u r) -> p x r u", x=2, u=2),
+                    out=tile[:, PIECE * n : PIECE * n + PIECE].bitcast(F32).rearrange("p (x m u) -> p x m u", x=2, u=2),
+                    in_=bank[:].rearrange("p (x u m) -> p x m u", x=2, u=2),
                 )
             grouped[key] = tile
-            if count == 2 and key not in parts:
-                load_next()
+            if key not in parts:
+                has_been_read(key)
 
         def quantize(src, place, width):
             code, scale, first = place
@@ -164,79 +178,88 @@ def tile_untied_position_value_gradient_s7_kernel(tc, q, k, pq, pk, g, go, out):
 
         def quantize_turn(key):
             name, digits = key.split(".")
-            width = len(digits) * PIECE
             src = grouped[key]
             if key in WIDE:
                 for c in range(2):
                     quantize(src[:, PIECE * c : PIECE * c + PIECE], columns["%s.%s" % (name, digits[0]), c], PIECE)
                 return
+            width = len(digits) * PIECE
             if ("%s.%s" % (name, digits[0]), 0) not in columns:
                 pair = code_tiles(key, width // PACK)
                 for n, d in enumerate(digits):
                     for x in range(2):
-                        columns["%s.%s" % (name, d), x] = pair + (256 * n + P * x,)
+                        columns["%s.%s" % (name, d), x] = pair + (P * (2 * n + x),)
             quantize(src[:, 0:width], columns["%s.%s" % (name, digits[0]), 0], width)
 
         def interleave(key, src, half, copy):
             if key not in grouped:
                 tile = work.tile([P, PACK * 512], BF16, name="interleaved", align_bytes=64, bufs=3)
                 grouped[key] = tile
-            cols = slice(256 * half, 256 * half + 256)
-            dst = grouped[key][:].rearrange("p (c t) -> p c t", t=PACK)
-            copy(out=dst[:, cols, :], in_=src.rearrange("p (t c) -> p c t", t=PACK)[:, cols, :])
+            quads = slice(64 * half, 64 * half + 64)
+            copy(
+                out=grouped[key][:].rearrange("p (c i s) -> p c s i", i=4, s=PACK)[:, quads],
+                in_=src.rearrange("p (s c i) -> p c s i", s=PACK, i=4)[:, quads],
+            )
 
         def mx(out_ap, lhs, rhs, n, start, stop):
-            lc, lscale, l0 = lhs
-            rc, rscale, r0 = rhs
+            lhs_code, lhs_scale, l0 = lhs
+            rhs_code, rhs_scale, r0 = rhs
             nc.tensor.matmul_mx(
                 out=out_ap,
-                lhsT=lc[:, l0 : l0 + P].bitcast(FP8X4),
-                lhsT_scale=lscale[:, l0 : l0 + P],
-                rhs=rc[:, r0 : r0 + n].bitcast(FP8X4),
-                rhs_scale=rscale[:, r0 : r0 + n],
+                lhsT=lhs_code[:, l0 : l0 + P].bitcast(FP8X4),
+                lhsT_scale=lhs_scale[:, l0 : l0 + P],
+                rhs=rhs_code[:, r0 : r0 + n].bitcast(FP8X4),
+                rhs_scale=rhs_scale[:, r0 : r0 + n],
                 start=start,
                 stop=stop,
             )
 
-        def stationary(b, h, t):
-            q_key, pq_key = "q%d%d.%d" % (b, h, t), "pq%d.%d" % (h, t // 2)
-            return [columns[q_key, 0], columns[q_key, 1], columns[pq_key, t % 2]]
+        def queries(b, h, s):
+            q_key, pq_key = "q%d%d.%d" % (b, h, s), "pq%d.%d" % (h, s // 2)
+            return [columns[q_key, 0], columns[q_key, 1], columns[pq_key, s % 2]]
 
         def score(b, h, j):
-            jh, r = divmod(j, 4)
+            half, s = divmod(j, PACK)
+            k_key, pk_key = "k%d%d.%d" % (b, half, s), "pk%d.%d" % (half, s // 2)
+            keys = [columns[k_key, 0], columns[k_key, 1], columns[pk_key, s % 2]]
             bank = psum.tile([P, 512], F32, name="bank")
-            k_key, pk_key = "k%d%d.%d" % (b, jh, r), "pk%d.%d" % (jh, r // 2)
-            moving = [columns[k_key, 0], columns[k_key, 1], columns[pk_key, r % 2]]
             for t in range(PACK):
-                for n, lhs in enumerate(stationary(b, h, t)):
-                    mx(bank[:, P * t : P * t + P], lhs, moving[n], P, n == 0, n == 2)
-            a_bf = work.tile([P, 512], BF16, name="a_bf", align_bytes=64, bufs=4)
+                for n, lhs in enumerate(queries(b, h, t)):
+                    mx(bank[:, P * t : P * t + P], lhs, keys[n], P, n == 0, n == 2)
+            banks[b, h, j] = bank
+
+        def gate_score(b, h, j):
+            tile = work.tile([P, 512], BF16, name="a_bf", align_bytes=64, bufs=4)
             nc.vector.scalar_tensor_tensor(
-                out=a_bf[:].rearrange("p (j t) -> p j t", t=PACK),
-                in0=bank[:].rearrange("p (t j) -> p j t", t=PACK),
+                out=tile[:].rearrange("p (j s) -> p j s", s=PACK),
+                in0=banks[b, h, j][:].rearrange("p (s j) -> p j s", s=PACK),
                 scalar=0.0,
                 in1=gate[b][1][:, h, :].unsqueeze(1).to_broadcast([P, P, PACK]),
                 op0=ALU.max,
                 op1=ALU.mult,
             )
-            grouped[b, h, j] = a_bf
+            grouped[b, h, j] = tile
 
         def quantize_a(b, h, j):
-            quantize(grouped[b, h, j][:], (codes["a%d%d" % (b, h)], scales["a%d%d" % (b, h)], P * j), 512)
+            key = "a%d%d" % (b, h)
+            quantize(grouped[b, h, j][:], (codes[key], scales[key], P * j), PACK * P)
 
-        def wide_score(b, h, jh, t):
+        def wide_score(b, h, half, s):
+            keys = [whole["k%d%d" % (b, half), 0], whole["k%d%d" % (b, half), 1], whole["pk%d" % half, 0]]
             bank = psum.tile([P, 512], F32, name="bank")
-            moving = [whole["k%d%d" % (b, jh), 0], whole["k%d%d" % (b, jh), 1], whole["pk%d" % jh, 0]]
-            for n, lhs in enumerate(stationary(b, h, t)):
-                mx(bank[:], lhs, moving[n], 512, n == 0, n == 2)
-            if t == 0:
+            for n, lhs in enumerate(queries(b, h, s)):
+                mx(bank[:], lhs, keys[n], 512, n == 0, n == 2)
+            banks[b, h, half, s] = bank
+
+        def gate_wide_score(b, h, half, s):
+            if s == 0:
                 tile = work.tile([P, PACK * 512], BF16, name="parted", align_bytes=64, bufs=7)
-                parted[b, h, jh] = tile
+                parted[b, h, half] = tile
             nc.vector.tensor_scalar(
-                out=parted[b, h, jh][:, 512 * t : 512 * t + 512],
-                in0=bank[:],
+                out=parted[b, h, half][:, 512 * s : 512 * s + 512],
+                in0=banks[b, h, half, s][:],
                 scalar1=0.0,
-                scalar2=gate[b][1][:, h, t : t + 1],
+                scalar2=gate[b][1][:, h, s : s + 1],
                 op0=ALU.max,
                 op1=ALU.mult,
             )
@@ -247,58 +270,71 @@ def tile_untied_position_value_gradient_s7_kernel(tc, q, k, pq, pk, g, go, out):
                 a_key, go_key = "a%d%d" % (b, h), "go%d%d" % (b, h)
                 mx(bank[:], (codes[a_key], scales[a_key], P * j), (codes[go_key], scales[go_key], 0), V, h == 0, h == 1)
             res = work.tile([P, V], F32, name="res", bufs=4)
-            jh, r = divmod(j, 4)
-            rows = out[b, 512 * jh : 512 * jh + 512, :].rearrange("(m r) v -> m r v", r=4)[:, r, :]
-            if (b, j) == (1, 7):
-                res2 = work.tile([P, V // 2], F32, name="res2", bufs=1)
+            half, s = divmod(j, PACK)
+            rows = out[b, HALF * half : HALF * half + HALF, :].rearrange("(m s) v -> m s v", s=PACK)[:, s, :]
+            if (b, j) == (B - 1, 7):
+                res_right = work.tile([P, V // 2], F32, name="res_right", bufs=1)
                 nc.scalar.copy(out=res[:, 0:256], in_=bank[:, 0:256])
-                nc.vector.tensor_copy(out=res2[:], in_=bank[:, 256:512])
+                nc.vector.tensor_copy(out=res_right[:], in_=bank[:, 256:512])
                 nc.sync.dma_start(out=rows[:, 0:256], in_=res[:, 0:256])
-                nc.sync.dma_start(out=rows[:, 256:512], in_=res2[:])
-            else:
-                copy = nc.vector.tensor_copy if "F%d%d" % (b, j) in OUT_ON_VECTOR else nc.scalar.copy
-                copy(out=res[:], in_=bank[:])
-                nc.sync.dma_start(out=rows, in_=res[:])
+                nc.sync.dma_start(out=rows[:, 256:512], in_=res_right[:])
+                return
+            copy = nc.vector.tensor_copy if "F%d%d" % (b, j) in OUT_ON_VECTOR else nc.scalar.copy
+            copy(out=res[:], in_=bank[:])
+            nc.sync.dma_start(out=rows, in_=res[:])
+
+        on_tensor = [s for s in steps if s in turns or s[0] in "SWF"]
+
+        def on_vector_behind(i):
+            turned = on_tensor[i - 1] if i > 0 else "-"
+            scored = on_tensor[i]
+            gated = on_tensor[i - 2] if i > 1 else "-"
+            if turned in turns:
+                quantize_turn(turned)
+            d = [int(c) for c in scored if c in "0123456789"]
+            if scored[0] == "S":
+                gate_score(d[0], d[1], d[2])
+            elif scored[0] == "W":
+                gate_wide_score(d[0], d[1], d[2], d[3])
+            if gated[0] == "S":
+                quantize_a(int(gated[1]), int(gated[2]), int(gated[3]))
 
         with tc.manual_schedule():
-            before = "-"
+            i = 0
             for step in steps:
                 kind = step[0]
                 d = [int(c) for c in step if c in "0123456789"]
                 if step[1] == ":":
                     part(step[2:], nc.vector.tensor_copy if kind == "P" else nc.scalar.copy)
-                    continue
-                if kind == "G":
+                elif kind in "GH":
                     key = "go" + step[1:3]
-                    interleave(key, raw[key][:], d[2], nc.scalar.copy)
-                    continue
-                if kind == "Q":
+                    second = key in grouped
+                    interleave(key, raw[key][:], d[2], nc.vector.tensor_copy if kind == "H" else nc.scalar.copy)
+                    if second:
+                        has_been_read(key)
+                elif kind == "Q":
                     key = "go" + step[1:3]
-                    load_next()
                     codes[key], scales[key] = code_tiles(key, V)
                     quantize(grouped[key][:], (codes[key], scales[key], 0), PACK * V)
-                    continue
-                if kind in "Ii":
-                    interleave(step[1:4], parted[d[0], d[1], d[2]][:], d[3], nc.vector.tensor_copy if kind == "I" else nc.scalar.copy)
-                    continue
-                if kind == "A":
-                    b, h, jh, half = d
+                elif kind in "Ii":
+                    slots = parted[d[0], d[1], d[2]]
+                    interleave(step[1:4], slots[:], d[3], nc.vector.tensor_copy if kind == "I" else nc.scalar.copy)
+                elif kind == "A":
+                    b, h, half, n = d
                     key = "a%d%d" % (b, h)
-                    quantize(grouped[step[1:4]][:, 1024 * half : 1024 * half + 1024], (codes[key], scales[key], 512 * jh + 256 * half), 1024)
-                    continue
-                if step in turns:
-                    turn(step)
-                elif kind == "S":
-                    if step == "S000":
-                        for gate_bf, gate_b in gate:
-                            nc.vector.tensor_copy(out=gate_b[:], in_=gate_bf[:])
-                    score(d[0], d[1], d[2])
-                elif kind == "W":
-                    wide_score(d[0], d[1], d[2], d[3])
-                elif kind == "F":
-                    gradient(d[0], d[1])
-                if before[0] == "S":
-                    quantize_a(int(before[1]), int(before[2]), int(before[3]))
-                elif before in turns:
-                    quantize_turn(before)
-                before = step
+                    place = (codes[key], scales[key], HALF * half + 256 * n)
+                    quantize(grouped[step[1:4]][:, PIECE * n : PIECE * n + PIECE], place, PIECE)
+                else:
+                    if step in turns:
+                        turn(step)
+                    elif kind == "S":
+                        if step == first_score:
+                            for gate_bf, gate_b in gate:
+                                nc.vector.tensor_copy(out=gate_b[:], in_=gate_bf[:])
+                        score(d[0], d[1], d[2])
+                    elif kind == "W":
+                        wide_score(d[0], d[1], d[2], d[3])
+                    else:
+                        gradient(d[0], d[1])
+                    on_vector_behind(i)
+                    i += 1

from contextlib import ExitStack

import concourse.mybir as mybir
from concourse.masks import make_identity

B, L, D, R, V = 2, 1024, 1024, 512, 512
FLOPS = 2 * (B * L * L * D + L * L * R + B * L * L * V)

F32 = mybir.dt.float32
BF16 = mybir.dt.bfloat16
U32 = mybir.dt.uint32
U8 = mybir.dt.uint8
FP8X4 = mybir.dt.float8_e4m3fn_x4
ALU = mybir.AluOpType

P = 128
PACK = 4
K_PASS = P * PACK
HALF = 512
PIECE = 1024
RING = 10

STEPS = (
    "P:q00.1 q00.0 pk0.0 k00.0 pq0.0 P:k00.1 q00.1 q00.2 pq0.1 q00.3 k00.1 pk0.1 pk1.01 k00.2 S000 S001 "
    "P:k00.3 P:pq1.01 q01.01 q01.23 k00.3 P:k01.23 pq1.01 k01.01 S002 k01.23 S003 G01.1 G00.0 S004 S005 S010 "
    "G00.1 S011 S012 G01.0 S013 S006 p:q10.01 S007 S014 Q00 p:q10.23 p:q11.01 P:k11.01 P:q11.23 P:k11.23 "
    "q10.01 k10.01 q10.23 k10.23 q11.01 q11.23 Q01 k11.01 k11.23 S015 G11.1 S016 S017 G10.1 W100.0 W100.1 "
    "G11.0 F00 F01 F02 W100.2 W100.3 G10.0 i100.0 W110.0 W110.1 F03 W110.2 W110.3 i100.1 Q10 W101.0 i110.0 "
    "A100.1 F04 W101.1 W101.2 W101.3 F05 A110.0 Q11 A100.0 i110.1 F06 i101.1 A110.1 S114 F07 i101.0 S115 F10 "
    "F11 A101.0 F12 A101.1 F13 S116 S117 F14 F15 F16 F17"
)
WIDE = ("k10.01", "k10.23", "k11.01", "k11.23")
OUT_ON_VECTOR = ("F07",)


def tile_untied_position_value_gradient_s7_kernel(tc, q, k, pq, pk, g, go, out):
    nc = tc.nc
    steps = STEPS.split()
    turns = [s for s in steps if s[0] in "qkp" and s[1] != ":"]
    parts = [s[2:] for s in steps if s[1] == ":"]
    first_score = [s for s in steps if s[0] == "S"][0]

    with ExitStack() as ctx:
        keep = ctx.enter_context(tc.tile_pool(name="keep", bufs=1))
        work = ctx.enter_context(tc.tile_pool(name="work", bufs=4))
        psum = ctx.enter_context(tc.psum_pool(name="psum", bufs=8))

        ident = keep.tile([P, P], F32, name="ident")
        make_identity(nc, ident[:])

        warm = keep.tile([P, 1], F32, name="warm")
        nc.vector.memset(warm[:], 0.0)
        nc.scalar.copy(out=warm[:], in_=warm[:])

        raw = {}
        parted = {}
        grouped = {}
        codes = {}
        scales = {}
        columns = {}
        banks = {}
        whole = {}
        gate = []

        def load(key):
            digits = key.split(".")[1] if "." in key else "01"
            if len(digits) == 1:
                tile = keep.tile([P, PIECE], BF16, name="raw_" + key, align_bytes=64)
            else:
                tile = work.tile([P, 2 * PIECE], BF16, name="raw", align_bytes=64, bufs=RING)
            if key[0] == "g":
                h = int(key[3])
                src = go[int(key[2]), HALF * h : HALF * h + HALF, :].rearrange("(p t) v -> p t v", t=PACK)
            else:
                name = key.split(".")[0]
                h = int(name[-1])
                rows = slice(HALF * h, HALF * h + HALF)
                if name[0] == "p":
                    src = (pq if name[1] == "q" else pk)[rows, :]
                    slots = 2
                else:
                    src = (q if name[0] == "q" else k)[int(name[1]), rows, :]
                    slots = 1
                first, last = slots * int(digits[0]), slots * int(digits[-1]) + slots
                src = src.rearrange("(m s) k -> m s k", s=PACK)[:, first:last, :]
            nc.sync.dma_start(out=tile[:].rearrange("p (s k) -> p s k", s=src.shape[1]), in_=src)
            raw[key] = tile

        pending = []
        for s in steps:
            if s in turns:
                pending.append(s)
            elif s[0] in "GH" and "go" + s[1:3] not in pending:
                pending.append("go" + s[1:3])
        singles = [s for s in turns if len(s.split(".")[1]) == 1]

        ring = []
        read = set()

        def load_next():
            if pending:
                key = pending.pop(0)
                load(key)
                if key not in singles:
                    ring.append(key)

        def has_been_read(key):
            read.add(key)
            while ring and ring[0] in read:
                ring.pop(0)
                load_next()

        for n in range(len(singles) + RING):
            load_next()
            if n == 7:
                for b in range(B):
                    gate_bf = keep.tile([P, 2, PACK], BF16, name="gate_bf_%d" % b)
                    nc.sync.dma_start(out=gate_bf[:], in_=g[b].rearrange("(h p s) -> p h s", p=P, s=PACK))
                    gate_b = keep.tile([P, 2, PACK], F32, name="gate_%d" % b)
                    gate.append((gate_bf, gate_b))

        def code_tiles(key, width):
            code = keep.tile([P, width], U32, name="codes_" + key, align_bytes=64)
            scale = keep.tile([P, width], U8, name="scales_" + key, align_bytes=64)
            return code, scale

        for b in range(B):
            for h in range(2):
                key = "a%d%d" % (b, h)
                codes[key], scales[key] = code_tiles(key, L)
        for name in ("k10", "k11"):
            pair = code_tiles(name, 2 * HALF)
            for c in range(2):
                whole[name, c] = pair + (HALF * c,)
                for s in range(PACK):
                    columns["%s.%d" % (name, s), c] = pair + (HALF * c + P * s,)
        for name in ("pk0", "pk1"):
            pair = code_tiles(name, HALF)
            whole[name, 0] = pair + (0,)
            for n in range(2):
                for x in range(2):
                    columns["%s.%d" % (name, n), x] = pair + (P * (2 * n + x),)

        def part(key, copy):
            pairs = len(key.split(".")[1]) * PIECE // 4
            tile = work.tile([P, 2, PIECE // 2], F32, name="parted", align_bytes=64, bufs=7)
            copy(
                out=tile[:, :, 0:pairs].rearrange("p u (c w) -> p c u w", c=2),
                in_=raw[key][:].bitcast(F32).rearrange("p (c w u) -> p c u w", c=2, u=2),
            )
            parted[key] = tile
            has_been_read(key)

        def turn(key):
            tile = work.tile([P, 2 * PIECE], BF16, name="grouped", align_bytes=64, bufs=4)
            for n in range(len(key.split(".")[1])):
                bank = psum.tile([P, 512], F32, name="bank")
                for x in range(2):
                    w = 2 * x + n if key in WIDE else 2 * n + x
                    for u in range(2):
                        if key in parts:
                            src = parted[key][:, u, P * w : P * w + P]
                        else:
                            src = raw[key][:].bitcast(F32)[:, 256 * w + u : 256 * w + 256 : 2]
                        nc.tensor.transpose(bank[:, 256 * x + P * u : 256 * x + P * u + P], src, ident[:])
                nc.scalar.copy(
                    out=tile[:, PIECE * n : PIECE * n + PIECE].bitcast(F32).rearrange("p (x m u) -> p x m u", x=2, u=2),
                    in_=bank[:].rearrange("p (x u m) -> p x m u", x=2, u=2),
                )
            grouped[key] = tile
            if key not in parts:
                has_been_read(key)

        def quantize(src, place, width):
            code, scale, first = place
            cols = slice(first, first + width // PACK)
            nc.vector.quantize_mx(out=code[:, cols].bitcast(FP8X4), scales=scale[:, cols], in_=src)

        def quantize_turn(key):
            name, digits = key.split(".")
            src = grouped[key]
            if key in WIDE:
                for c in range(2):
                    quantize(src[:, PIECE * c : PIECE * c + PIECE], columns["%s.%s" % (name, digits[0]), c], PIECE)
                return
            width = len(digits) * PIECE
            if ("%s.%s" % (name, digits[0]), 0) not in columns:
                pair = code_tiles(key, width // PACK)
                for n, d in enumerate(digits):
                    for x in range(2):
                        columns["%s.%s" % (name, d), x] = pair + (P * (2 * n + x),)
            quantize(src[:, 0:width], columns["%s.%s" % (name, digits[0]), 0], width)

        def interleave(key, src, half, copy):
            if key not in grouped:
                tile = work.tile([P, PACK * 512], BF16, name="interleaved", align_bytes=64, bufs=3)
                grouped[key] = tile
            quads = slice(64 * half, 64 * half + 64)
            copy(
                out=grouped[key][:].rearrange("p (c i s) -> p c s i", i=4, s=PACK)[:, quads],
                in_=src.rearrange("p (s c i) -> p c s i", s=PACK, i=4)[:, quads],
            )

        def mx(out_ap, lhs, rhs, n, start, stop):
            lhs_code, lhs_scale, l0 = lhs
            rhs_code, rhs_scale, r0 = rhs
            nc.tensor.matmul_mx(
                out=out_ap,
                lhsT=lhs_code[:, l0 : l0 + P].bitcast(FP8X4),
                lhsT_scale=lhs_scale[:, l0 : l0 + P],
                rhs=rhs_code[:, r0 : r0 + n].bitcast(FP8X4),
                rhs_scale=rhs_scale[:, r0 : r0 + n],
                start=start,
                stop=stop,
            )

        def queries(b, h, s):
            q_key, pq_key = "q%d%d.%d" % (b, h, s), "pq%d.%d" % (h, s // 2)
            return [columns[q_key, 0], columns[q_key, 1], columns[pq_key, s % 2]]

        def score(b, h, j):
            half, s = divmod(j, PACK)
            k_key, pk_key = "k%d%d.%d" % (b, half, s), "pk%d.%d" % (half, s // 2)
            keys = [columns[k_key, 0], columns[k_key, 1], columns[pk_key, s % 2]]
            bank = psum.tile([P, 512], F32, name="bank")
            for t in range(PACK):
                for n, lhs in enumerate(queries(b, h, t)):
                    mx(bank[:, P * t : P * t + P], lhs, keys[n], P, n == 0, n == 2)
            banks[b, h, j] = bank

        def gate_score(b, h, j):
            tile = work.tile([P, 512], BF16, name="a_bf", align_bytes=64, bufs=4)
            nc.vector.scalar_tensor_tensor(
                out=tile[:].rearrange("p (j s) -> p j s", s=PACK),
                in0=banks[b, h, j][:].rearrange("p (s j) -> p j s", s=PACK),
                scalar=0.0,
                in1=gate[b][1][:, h, :].unsqueeze(1).to_broadcast([P, P, PACK]),
                op0=ALU.max,
                op1=ALU.mult,
            )
            grouped[b, h, j] = tile

        def quantize_a(b, h, j):
            key = "a%d%d" % (b, h)
            quantize(grouped[b, h, j][:], (codes[key], scales[key], P * j), PACK * P)

        def wide_score(b, h, half, s):
            keys = [whole["k%d%d" % (b, half), 0], whole["k%d%d" % (b, half), 1], whole["pk%d" % half, 0]]
            bank = psum.tile([P, 512], F32, name="bank")
            for n, lhs in enumerate(queries(b, h, s)):
                mx(bank[:], lhs, keys[n], 512, n == 0, n == 2)
            banks[b, h, half, s] = bank

        def gate_wide_score(b, h, half, s):
            if s == 0:
                tile = work.tile([P, PACK * 512], BF16, name="parted", align_bytes=64, bufs=7)
                parted[b, h, half] = tile
            nc.vector.tensor_scalar(
                out=parted[b, h, half][:, 512 * s : 512 * s + 512],
                in0=banks[b, h, half, s][:],
                scalar1=0.0,
                scalar2=gate[b][1][:, h, s : s + 1],
                op0=ALU.max,
                op1=ALU.mult,
            )

        def gradient(b, j):
            bank = psum.tile([P, V], F32, name="bank")
            for h in range(2):
                a_key, go_key = "a%d%d" % (b, h), "go%d%d" % (b, h)
                mx(bank[:], (codes[a_key], scales[a_key], P * j), (codes[go_key], scales[go_key], 0), V, h == 0, h == 1)
            res = work.tile([P, V], F32, name="res", bufs=4)
            half, s = divmod(j, PACK)
            rows = out[b, HALF * half : HALF * half + HALF, :].rearrange("(m s) v -> m s v", s=PACK)[:, s, :]
            if (b, j) == (B - 1, 7):
                res_right = work.tile([P, V // 2], F32, name="res_right", bufs=1)
                nc.scalar.copy(out=res[:, 0:256], in_=bank[:, 0:256])
                nc.vector.tensor_copy(out=res_right[:], in_=bank[:, 256:512])
                nc.sync.dma_start(out=rows[:, 0:256], in_=res[:, 0:256])
                nc.sync.dma_start(out=rows[:, 256:512], in_=res_right[:])
                return
            copy = nc.vector.tensor_copy if "F%d%d" % (b, j) in OUT_ON_VECTOR else nc.scalar.copy
            copy(out=res[:], in_=bank[:])
            nc.sync.dma_start(out=rows, in_=res[:])

        on_tensor = [s for s in steps if s in turns or s[0] in "SWF"]

        def on_vector_behind(i):
            turned = on_tensor[i - 1] if i > 0 else "-"
            scored = on_tensor[i]
            gated = on_tensor[i - 2] if i > 1 else "-"
            if turned in turns:
                quantize_turn(turned)
            d = [int(c) for c in scored if c in "0123456789"]
            if scored[0] == "S":
                gate_score(d[0], d[1], d[2])
            elif scored[0] == "W":
                gate_wide_score(d[0], d[1], d[2], d[3])
            if gated[0] == "S":
                quantize_a(int(gated[1]), int(gated[2]), int(gated[3]))

        with tc.manual_schedule():
            i = 0
            for step in steps:
                kind = step[0]
                d = [int(c) for c in step if c in "0123456789"]
                if step[1] == ":":
                    part(step[2:], nc.vector.tensor_copy if kind == "P" else nc.scalar.copy)
                elif kind in "GH":
                    key = "go" + step[1:3]
                    second = key in grouped
                    interleave(key, raw[key][:], d[2], nc.vector.tensor_copy if kind == "H" else nc.scalar.copy)
                    if second:
                        has_been_read(key)
                elif kind == "Q":
                    key = "go" + step[1:3]
                    codes[key], scales[key] = code_tiles(key, V)
                    quantize(grouped[key][:], (codes[key], scales[key], 0), PACK * V)
                elif kind in "Ii":
                    slots = parted[d[0], d[1], d[2]]
                    interleave(step[1:4], slots[:], d[3], nc.vector.tensor_copy if kind == "I" else nc.scalar.copy)
                elif kind == "A":
                    b, h, half, n = d
                    key = "a%d%d" % (b, h)
                    place = (codes[key], scales[key], HALF * half + 256 * n)
                    quantize(grouped[step[1:4]][:, PIECE * n : PIECE * n + PIECE], place, PIECE)
                else:
                    if step in turns:
                        turn(step)
                    elif kind == "S":
                        if step == first_score:
                            for gate_bf, gate_b in gate:
                                nc.vector.tensor_copy(out=gate_b[:], in_=gate_bf[:])
                        score(d[0], d[1], d[2])
                    elif kind == "W":
                        wide_score(d[0], d[1], d[2], d[3])
                    else:
                        gradient(d[0], d[1])
                    on_vector_behind(i)
                    i += 1
